import numpy as np, ml_dtypes
CORES = [0,1,2,3]
N = 4
ROOT = 3
def setup_inputs(rng):
    return {"x": rng.standard_normal((N, 128, 8), dtype=np.float32).astype(ml_dtypes.bfloat16)}
def reference(x):
    y = np.full((N, 128, N * 8), np.nan, x.dtype)
    y[ROOT] = np.concatenate(list(x), axis=1)
    return {"y": y}

SCRATCH = {
    "stage": ("sbuf", [128, 8], "bfloat16"),
    "land": ("sbuf", [128, 32], "bfloat16"),
}
SEMAPHORES = ["loaded", "read", "arrived", "stored"]


def rank_program(g, core, T, topo):
    rank = T.rank_of(core)
    if rank is None:
        return
    n = len(T.cores)
    root = T.root if T.root is not None else n - 1
    root_core = T.cores[root]
    w = T.x.shape[1]

    def engines(src):
        m = topo.mask(src, root_core)
        return m, bin(m).count("1")

    if rank != root:
        g.dma_start(T.stage[:], T.x[:]).then_inc(T.sem.loaded, 16)
        g.wait_ge(T.sem.loaded, 16)
        m, k = engines(core)
        rid, pid, sengine = topo.addr(root_core)
        g.remote_dma(T.land[:, rank * w:(rank + 1) * w], T.stage[:], T.sem.arrived, T.sem.read, pid, rid, m)
        g.wait_ge(T.sem.read, k)
        return

    g.dma_start(T.land[:, root * w:(root + 1) * w], T.x[:]).then_inc(T.sem.loaded, 16)
    g.wait_ge(T.sem.loaded, 16)
    total = sum(engines(c)[1] for c in T.cores if c != root_core)
    g.wait_ge(T.sem.arrived, total)
    g.dma_start(T.y[:], T.land[:]).then_inc(T.sem.stored, 16)
    g.wait_ge(T.sem.stored, 16)
